import numpy as np
import ml_dtypes


def mxq(x, axis, fmt="e4m3"):
    dtype, down = {"e4m3": (ml_dtypes.float8_e4m3fn, 7), "e5m2": (ml_dtypes.float8_e5m2, 14)}[fmt]
    v = np.moveaxis(np.asarray(x, np.float32).astype(ml_dtypes.bfloat16).astype(np.float64), axis, -1)
    blocks = v.reshape(v.shape[:-1] + (-1, 32))
    amax = np.abs(blocks).max(-1, keepdims=True)
    byte = np.maximum(np.where(amax > 0, np.frexp(amax)[1] - 1 + 127, 0) - down, 1)
    scale = np.exp2(byte - 127.0)
    codes = (blocks / scale).astype(np.float32).astype(dtype).astype(np.float64)
    return np.moveaxis((codes * scale).reshape(v.shape), -1, axis)


WIDE = False


def mx_kscale(k):
    if not WIDE:
        return np.ones(k)
    levels = np.array([10, -10, 5, -5, 0])
    if k % 512:
        return np.exp2(np.random.permutation(np.resize(levels, k // 32))).repeat(32)
    a = np.empty((k // 512, 16))
    for p in range(k // 512):
        a[p, :8] = np.random.permutation(np.resize(levels, 8))
        for g in range(8):
            far = levels[np.abs(levels - a[p, g]) >= 10]
            a[p, g + 8] = far[np.random.randint(len(far))]
    return np.exp2(a.ravel()).repeat(32)


def f64(x):
    return np.asarray(x).astype(np.float64)


def striped(idx):
    return np.tile(np.asarray(idx).reshape(-1, 16).T, (8, 1)).astype(np.uint16)


def unstriped(offs):
    return offs[:16].T.reshape(-1).astype(np.int64)


E2M1 = np.array([0.0, 0.5, 1.0, 1.5, 2.0, 3.0, 4.0, 6.0, -0.0, -0.5, -1.0, -1.5, -2.0, -3.0, -4.0, -6.0])


def pack_weight(w, fmt):
    k, n = w.shape
    w = f64(np.asarray(w, np.float32).astype(ml_dtypes.bfloat16)).reshape(k // 32, 32, n)
    amax = np.abs(w).max(1)
    if fmt == "e4m3":
        byte = np.frexp(amax)[1] - 1 + 127 - 7
    else:
        mant, ex = np.frexp(amax / 6.0)
        byte = np.where(mant > 0.5, ex, ex - 1) + 127
    byte = np.clip(np.where(amax > 0, byte, 1), 1, 254)
    scaled = (w * np.exp2(127.0 - byte)[:, None, :]).reshape(k, n).astype(np.float32)
    by_word = np.ascontiguousarray(scaled.reshape(k // 512, 128, 4, n).transpose(0, 1, 3, 2))
    if fmt == "e4m3":
        words = by_word.astype(ml_dtypes.float8_e4m3fn).view(np.uint8)
    else:
        c = by_word.astype(ml_dtypes.float4_e2m1fn).view(np.uint8) & 0xF
        words = (c[..., 0::2] | (c[..., 1::2] << 4)).reshape(k // 512, 128, 2 * n)
    return np.ascontiguousarray(words), np.ascontiguousarray(byte.astype(np.uint8).reshape(k // 512, 16, n))


def unpack_weight(words, scales, fmt):
    g, _, n = scales.shape
    words = np.ascontiguousarray(words).reshape(g, 128, n, -1)
    if fmt == "e4m3":
        vals = words.view(ml_dtypes.float8_e4m3fn).astype(np.float64)
    else:
        nib = np.empty((g, 128, n, 4), np.uint8)
        nib[..., 0::2] = words & 0xF
        nib[..., 1::2] = words >> 4
        vals = E2M1[nib]
    vals = vals * np.repeat(np.exp2(scales.astype(np.float64) - 127.0), 8, axis=1)[..., None]
    return vals.transpose(0, 1, 3, 2).reshape(g * 512, n)


def bf(x):
    return np.asarray(x, np.float32).astype(ml_dtypes.bfloat16)


def planes(Y):
    r, m = Y.shape
    b = f64(bf(Y)).reshape(r // 32, 32, m)
    amax = np.abs(b).max(1)
    byte = np.clip(np.where(amax > 0, np.frexp(amax)[1] - 1 + 127 - 7, 1), 1, 254)
    codes = (b * np.exp2(127.0 - byte)[:, None, :]).reshape(r, m).astype(np.float32).astype(ml_dtypes.float8_e4m3fn).view(np.uint8)
    words = codes.reshape(r // 512, 128, 4, m).transpose(0, 1, 3, 2)
    return np.ascontiguousarray(words), np.ascontiguousarray(byte.astype(np.uint8).reshape(r // 512, 16, m))


D, T, I, Q, E, G = 512, 2048, 512, 256, 512, 64


def setup_inputs():
    n = np.random.standard_normal
    idx = np.random.permutation(T)[:I]
    fd = mx_kscale(D)
    fi = mx_kscale(I)
    ti = np.ones(T)
    ti[idx] = fi
    keysp = pack_weight(n((D, T)) / fd[:, None], "e2m1")
    return {
        "query": (n((D, Q)) * 0.8 / np.sqrt(D) * fd[:, None]).astype(np.float32),
        "keys_words": keysp[0],
        "keys_scales": keysp[1],
        "lam": (np.random.uniform(0.3, 0.9, (1, Q))).astype(np.float32),
        "bar": (np.random.uniform(0.6, 1.0, (Q, 1))).astype(np.float32),
        "reserve": (np.random.uniform(20.0, 80.0, (Q, 1))).astype(np.float32),
        "os": (np.random.uniform(4.0, 16.0, (1, I)) * fi).astype(np.float32),
        "vals": (n((E, T)) / ti).astype(np.float32),
        "floors": (n((E, Q)) * 1.5).astype(np.float32),
        "offs": striped(idx),
    }


def reference(query, keys_words, keys_scales, lam, bar, reserve, os, vals, floors, offs):
    idx = unstriped(offs)
    keysu = unpack_weight(keys_words, keys_scales, "e2m1")
    keysidxg = keysu[:, idx]
    queryq = mxq(f64(query), 0, "e4m3")
    a0 = keysidxg.T @ queryq
    a1p = np.pad(a0, ((0, 0), (1, 0)))[:, :Q]
    s0 = a0 + np.tanh(a1p) * f64(lam)
    s = s0.T
    p = np.exp(s)
    pm = p.reshape(Q, G, I // G).mean(axis=2)
    pr = np.repeat(pm, I // G, axis=1)
    r = np.maximum(p - pr * f64(bar), 0.0)
    w = r / (np.sum(r, axis=1, keepdims=True) + f64(reserve))
    wo1 = w * f64(os)
    wt1 = wo1.T
    vt1 = f64(vals)[:, idx].T
    vt1q = mxq(vt1, 0, "e4m3")
    wt1q = mxq(wt1, 0, "e4m3")
    o = vt1q.T @ wt1q
    y = np.maximum(o, f64(floors)) + np.minimum(o, f64(floors)) * 0.1
    words, scales = planes(y)
    return y, words, scales

@@ -1,0 +1,231 @@
+from contextlib import ExitStack
+
+import concourse.mybir as mybir
+from concourse.masks import make_identity
+
+D, T, I, Q, E, G = 512, 2048, 512, 256, 512, 64
+RUN = I // G
+P = 128
+PACK = 4
+FLOPS = 2 * D * I * Q + 2 * I * E * Q
+
+F32 = mybir.dt.float32
+BF16 = mybir.dt.bfloat16
+I32 = mybir.dt.int32
+U32 = mybir.dt.uint32
+U16 = mybir.dt.uint16
+U8 = mybir.dt.uint8
+FP8X4 = mybir.dt.float8_e4m3fn_x4
+FP4X4 = mybir.dt.float4_e2m1fn_x4
+ALU = mybir.AluOpType
+ACT = mybir.ActivationFunctionType
+AX = mybir.AxisListType
+
+EVEN, ODD, BEFORE = 0, 1, 2
+CAST_SPLIT = 160
+
+
+def tile_attend_afterprevious_abovepage_atleast_pl_kernel(
+    tc, query, keys_words, keys_scales, lam, bar, reserve, slot_factor, vals, floors, offs, out_0, out_1, out_2
+):
+    nc = tc.nc
+    with ExitStack() as ctx:
+        sb = ctx.enter_context(tc.tile_pool(name="sb", bufs=1))
+        ps = ctx.enter_context(tc.psum_pool(name="ps", bufs=1))
+
+        def bank(b, shape, name):
+            return ps.tile(shape, F32, name=name, tag="bank%d" % b)
+
+        offsets = sb.tile([P, I // 16], U16, name="offsets")
+        key_scale_pool = sb.tile([P, T], U8, name="key_scale_pool")
+        key_word_pool = sb.tile([P, T], U16, name="key_word_pool")
+        q_raw = sb.tile([P, PACK, Q], F32, name="q_raw")
+        val_pool = [sb.tile([P, T], F32, name="val_pool%d" % t) for t in range(PACK)]
+        floor_sb = [sb.tile([P, 2, Q], F32, name="floor_sb%d" % a) for a in range(2)]
+        floor_tenth = [sb.tile([P, Q], F32, name="floor_tenth%d" % t) for t in range(PACK)]
+        lam_sb = sb.tile([P, 2], F32, name="lam_sb")
+        bar_sb = sb.tile([P, 2], F32, name="bar_sb")
+        reserve_sb = sb.tile([P, 2], F32, name="reserve_sb")
+        factor_sb = sb.tile([P, PACK], F32, name="factor_sb")
+        val_rows = vals.rearrange("(p t) n -> t p n", t=PACK)
+        nc.gpsimd.memset(key_scale_pool[:].bitcast(I32), 0)
+        nc.sync.dma_start(offsets[:], offs)
+        for quad in range(4):
+            nc.sync.dma_start(
+                out=key_scale_pool[32 * quad : 32 * quad + 4, :].bitcast(I32),
+                in_=keys_scales[0, 4 * quad : 4 * quad + 4, :].bitcast(I32),
+            )
+        nc.sync.dma_start(out=key_word_pool[:].bitcast(I32), in_=keys_words[0].bitcast(I32))
+        nc.sync.dma_start(out=q_raw[:], in_=query.rearrange("(p j) q -> p j q", j=PACK))
+        nc.sync.dma_start(out=lam_sb[:], in_=lam.rearrange("o (p h) -> (o p) h", h=2))
+        nc.sync.dma_start(out=val_pool[0][:], in_=val_rows[0])
+        nc.sync.dma_start(out=bar_sb[:], in_=bar.rearrange("(p h) o -> p (h o)", h=2))
+        nc.sync.dma_start(out=factor_sb[:], in_=slot_factor.rearrange("o (p t) -> (o p) t", t=PACK))
+        nc.sync.dma_start(out=reserve_sb[:], in_=reserve.rearrange("(p h) o -> p (h o)", h=2))
+        for t in range(1, PACK):
+            nc.sync.dma_start(out=val_pool[t][:], in_=val_rows[t])
+        floor_rows = floors.rearrange("(p a b) q -> a p b q", a=2, b=2)
+        for a in range(2):
+            nc.sync.dma_start(out=floor_sb[a][:], in_=floor_rows[a])
+        ident = sb.tile([P, P], F32, name="ident")
+        make_identity(nc, ident[:])
+        neg_bar = sb.tile([P, 2], F32, name="neg_bar")
+        nc.gpsimd.tensor_scalar(neg_bar[:], bar_sb[:], -1.0 / RUN, 0.0, ALU.mult, ALU.add)
+
+        key_scales = sb.tile([P, I], U8, name="key_scales", align_bytes=64)
+        key_words = sb.tile([P, I], U16, name="key_words", align_bytes=64)
+        nc.vector.tensor_copy(key_scales[:], key_scale_pool[:].indirect(offsets[:]))
+        nc.vector.tensor_copy(key_words[:], key_word_pool[:].indirect(offsets[:]))
+
+        q_bf = [sb.tile([P, P, PACK], BF16, name="q_bf%d" % k, align_bytes=64) for k in range(3)]
+        q_codes = [sb.tile([P, P], U32, name="q_codes%d" % k, align_bytes=64) for k in range(3)]
+        q_scales = [sb.tile([P, P], U8, name="q_scales%d" % k, align_bytes=64) for k in range(3)]
+        q_pairs = q_raw[:].rearrange("p j (m h) -> p h m j", h=2)
+        nc.gpsimd.memset(q_bf[BEFORE][:, 0, :], 0.0)
+        nc.scalar.activation(q_bf[EVEN][:], q_pairs[:, EVEN], ACT.Copy)
+        nc.scalar.activation(q_bf[ODD][:], q_pairs[:, ODD], ACT.Copy)
+        nc.gpsimd.tensor_scalar(q_bf[BEFORE][:, 1:, :], q_pairs[:, ODD, : P - 1, :], 1.0, 0.0, ALU.mult, ALU.add)
+        scores = []
+        for k in range(3):
+            nc.vector.quantize_mx(
+                out=q_codes[k][:].bitcast(FP8X4), scales=q_scales[k][:], in_=q_bf[k][:].rearrange("p m j -> p (m j)")
+            )
+            score = bank(k, [P, I], "score%d" % k)
+            nc.tensor.matmul_mx(
+                out=score[:],
+                lhsT=q_codes[k][:].bitcast(FP8X4),
+                lhsT_scale=q_scales[k][:],
+                rhs=key_words[:].bitcast(FP4X4),
+                rhs_scale=key_scales[:],
+                start=True,
+                stop=True,
+            )
+            scores.append(score)
+
+        factor_ps = bank(3, [P, PACK, P], "factor_ps")
+        for t in range(PACK):
+            nc.tensor.transpose(factor_ps[:, t, :], factor_sb[:, t : t + 1].to_broadcast([P, P]), ident[:])
+
+        def per_parity(name, shape, dtype):
+            return [sb.tile(shape, dtype, name="%s%d" % (name, h), tag="%s%d" % (name, h), align_bytes=64) for h in range(2)]
+
+        th = per_parity("th", [P, I], F32)
+        s = per_parity("s", [P, I], F32)
+        p = per_parity("p", [P, I], F32)
+        run_sum = per_parity("run_sum", [P, G], F32)
+        excess = per_parity("excess", [P, I], F32)
+        part = per_parity("part", [P, I], F32)
+        part_sum = per_parity("part_sum", [P, 1], F32)
+        denom = per_parity("denom", [P, 1], F32)
+        recip = per_parity("recip", [P, 1], F32)
+        w_rows = per_parity("w_rows", [P, I], BF16)
+        w_turned = per_parity("w_turned", [P, P, 2], F32)
+        w_codes = sb.tile([P, Q], U32, name="w_codes", align_bytes=64)
+        w_scales = sb.tile([P, Q], U8, name="w_scales", align_bytes=64)
+        previous = {ODD: EVEN, EVEN: BEFORE}
+        order = (ODD, EVEN)
+
+        def turn_words(rows, b, dest, name, copy):
+            words = rows[:].bitcast(F32)
+            turned = bank(b, [P, 2, P], name)
+            for u in range(2):
+                nc.tensor.transpose(turned[:, u, :], words[:, u : I // 2 : 2], ident[:])
+            copy(dest[:], turned[:].rearrange("s u x -> s x u"))
+
+        for h in order:
+            nc.scalar.activation(th[h][:], scores[previous[h]][:], ACT.Tanh)
+            nc.vector.scalar_tensor_tensor(s[h][:], th[h][:], lam_sb[:, h : h + 1], scores[h][:], ALU.mult, ALU.add)
+        for h in order:
+            nc.scalar.activation(p[h][:], s[h][:], ACT.Exp)
+        for h in order:
+            nc.vector.tensor_reduce(run_sum[h][:], p[h][:].rearrange("q (g r) -> q g r", r=RUN), AX.X, ALU.add)
+        for h in order:
+            nc.vector.scalar_tensor_tensor(
+                excess[h][:].rearrange("q (g r) -> q g r", r=RUN),
+                run_sum[h][:].unsqueeze(2).to_broadcast([P, G, RUN]),
+                neg_bar[:, h : h + 1],
+                p[h][:].rearrange("q (g r) -> q g r", r=RUN),
+                ALU.mult,
+                ALU.add,
+            )
+            nc.scalar.activation(part[h][:], excess[h][:], ACT.Relu, accum_out=part_sum[h][:])
+        for h in order:
+            nc.vector.tensor_tensor(denom[h][:], part_sum[h][:], reserve_sb[:, h : h + 1], ALU.add)
+            nc.vector.reciprocal(recip[h][:], denom[h][:])
+            nc.vector.scalar_tensor_tensor(
+                w_rows[h][:].rearrange("q (x t) -> q x t", t=PACK),
+                part[h][:].rearrange("q (x t) -> q x t", t=PACK),
+                recip[h][:],
+                factor_ps[:].rearrange("q t x -> q x t"),
+                ALU.mult,
+                ALU.mult,
+            )
+            turn_words(w_rows[h], previous[h] + 1 if h == ODD else BEFORE, w_turned[h], "w_ps%d" % h, nc.scalar.copy if h == ODD else nc.vector.tensor_copy)
+            nc.vector.quantize_mx(
+                out=w_codes[:, h * P : (h + 1) * P].bitcast(FP8X4),
+                scales=w_scales[:, h * P : (h + 1) * P],
+                in_=w_turned[h][:].rearrange("s x u -> s (x u)").bitcast(BF16),
+            )
+
+        reuse = ["v_rows0", "s%d" % EVEN, "excess%d" % EVEN, "part%d" % EVEN]
+        v_rows = [sb.tile([P, I], BF16, name="v_rows%d" % t, tag=reuse[t], align_bytes=64) for t in range(PACK)]
+        v_turned = [sb.tile([P, P, 2], F32, name="v_turned%d" % t, align_bytes=64) for t in range(PACK)]
+        v_codes = [sb.tile([P, P], U32, name="v_codes%d" % t, align_bytes=64) for t in range(PACK)]
+        v_scales = [sb.tile([P, P], U8, name="v_scales%d" % t, align_bytes=64) for t in range(PACK)]
+        half = I // 2
+        for t in range(PACK):
+            if t == 2:
+                nc.scalar.activation(v_rows[t][:], val_pool[t][:].indirect(offsets[:]), ACT.Copy)
+            else:
+                nc.vector.tensor_copy(v_rows[t][:, :half], val_pool[t][:].indirect(offsets[:, : half // 16]))
+                nc.scalar.activation(v_rows[t][:, half:], val_pool[t][:].indirect(offsets[:, half // 16 :]), ACT.Copy)
+            turn_words(v_rows[t], 4 + t, v_turned[t], "v_ps%d" % t, nc.scalar.copy)
+            nc.vector.quantize_mx(
+                out=v_codes[t][:].bitcast(FP8X4),
+                scales=v_scales[t][:],
+                in_=v_turned[t][:].rearrange("s x u -> s (x u)").bitcast(BF16),
+            )
+
+        y = sb.tile([P, PACK, Q], F32, name="y")
+        out_rows = out_0.rearrange("(p t) q -> t p q", t=PACK)
+        for t in range(PACK):
+            o = bank(t, [P, 2, P], "o%d" % t)
+            nc.tensor.matmul_mx(
+                out=o[:].rearrange("e h m -> e (h m)"),
+                lhsT=v_codes[t][:].bitcast(FP8X4),
+                lhsT_scale=v_scales[t][:],
+                rhs=w_codes[:].bitcast(FP8X4),
+                rhs_scale=w_scales[:],
+                start=True,
+                stop=True,
+            )
+            o_nat = o[:].rearrange("e h m -> e m h")
+            f_row = floor_sb[t // 2][:, t % 2, :]
+            nc.gpsimd.tensor_scalar(floor_tenth[t][:], f_row, 0.1, 0.0, ALU.mult, ALU.add)
+            f_nat = f_row.rearrange("e (m h) -> e m h", h=2)
+            f_tenth = floor_tenth[t][:].rearrange("e (m h) -> e m h", h=2)
+            above = sb.tile([P, P, 2], F32, name="above%d" % t)
+            below = sb.tile([P, P, 2], F32, name="below%d" % t)
+            nc.vector.tensor_tensor(above[:], o_nat, f_nat, ALU.max)
+            nc.vector.scalar_tensor_tensor(below[:], o_nat, 0.1, f_tenth, ALU.mult, ALU.min)
+            (nc.gpsimd if t < PACK - 1 else nc.vector).tensor_tensor(
+                y[:, t, :], above[:].rearrange("e m h -> e (m h)"), below[:].rearrange("e m h -> e (m h)"), ALU.add
+            )
+            nc.sync.dma_start(out=out_rows[t], in_=y[:, t, :])
+
+        y_bf = sb.tile([P, Q, PACK], BF16, name="y_bf", align_bytes=64)
+        y_codes = sb.tile([P, Q], U32, name="y_codes", align_bytes=64)
+        y_scales = sb.tile([P, Q], U8, name="y_scales", align_bytes=64)
+        y_cols = y[:].rearrange("p t q -> p q t")
+        nc.vector.tensor_copy(y_bf[:, :CAST_SPLIT, :], y_cols[:, :CAST_SPLIT, :])
+        nc.scalar.copy(y_bf[:, CAST_SPLIT:, :], y_cols[:, CAST_SPLIT:, :])
+        nc.vector.quantize_mx(
+            out=y_codes[:].bitcast(FP8X4), scales=y_scales[:], in_=y_bf[:].rearrange("p q t -> p (q t)")
+        )
+        nc.sync.dma_start(out=out_1[0].rearrange("p c r -> p (c r)").bitcast(I32), in_=y_codes[:].bitcast(I32))
+        for quad in range(4):
+            queue = nc.scalar if quad % 2 == 0 else nc.sync
+            queue.dma_start(
+                out=out_2[0, 4 * quad : 4 * quad + 4, :].bitcast(I32),
+                in_=y_scales[32 * quad : 32 * quad + 4, :].bitcast(I32),
+            )

@@ -23,6 +23,17 @@ AX = mybir.AxisListType
 
 EVEN, ODD, BEFORE = 0, 1, 2
 CAST_SPLIT = 160
+HALVES = 2
+EARLY = False
+RELU = "SV"
+GATHER = ["VS","S","S","S"]
+HOLD = [None,None,None,None]
+WCOPY = "VS"
+VCOPY = "SVVS"
+ADDS = "VVVV"
+DEN = "S"
+EXCESS = "VV"
+KEYS_FIRST = True
 
 
 def tile_attend_afterprevious_abovepage_atleast_pl_kernel(
@@ -36,13 +47,16 @@ def tile_attend_afterprevious_abovepage_atleast_pl_kernel(
         def bank(b, shape, name):
             return ps.tile(shape, F32, name=name, tag="bank%d" % b)
 
+        def copier(e):
+            return nc.scalar.copy if e == "S" else nc.vector.tensor_copy
+
         offsets = sb.tile([P, I // 16], U16, name="offsets")
         key_scale_pool = sb.tile([P, T], U8, name="key_scale_pool")
         key_word_pool = sb.tile([P, T], U16, name="key_word_pool")
         q_raw = sb.tile([P, PACK, Q], F32, name="q_raw")
         val_pool = [sb.tile([P, T], F32, name="val_pool%d" % t) for t in range(PACK)]
         floor_sb = [sb.tile([P, 2, Q], F32, name="floor_sb%d" % a) for a in range(2)]
-        floor_tenth = [sb.tile([P, Q], F32, name="floor_tenth%d" % t) for t in range(PACK)]
+        floor_tenth = [sb.tile([P, 2, Q], F32, name="floor_tenth%d" % a) for a in range(2)]
         lam_sb = sb.tile([P, 2], F32, name="lam_sb")
         bar_sb = sb.tile([P, 2], F32, name="bar_sb")
         reserve_sb = sb.tile([P, 2], F32, name="reserve_sb")
@@ -55,10 +69,13 @@ def tile_attend_afterprevious_abovepage_atleast_pl_kernel(
                 out=key_scale_pool[32 * quad : 32 * quad + 4, :].bitcast(I32),
                 in_=keys_scales[0, 4 * quad : 4 * quad + 4, :].bitcast(I32),
             )
-        nc.sync.dma_start(out=key_word_pool[:].bitcast(I32), in_=keys_words[0].bitcast(I32))
-        nc.sync.dma_start(out=q_raw[:], in_=query.rearrange("(p j) q -> p j q", j=PACK))
-        nc.sync.dma_start(out=lam_sb[:], in_=lam.rearrange("o (p h) -> (o p) h", h=2))
+        for keys_now in (KEYS_FIRST, not KEYS_FIRST):
+            if keys_now:
+                nc.sync.dma_start(out=key_word_pool[:].bitcast(I32), in_=keys_words[0].bitcast(I32))
+            else:
+                nc.sync.dma_start(out=q_raw[:], in_=query.rearrange("(p j) q -> p j q", j=PACK))
         nc.sync.dma_start(out=val_pool[0][:], in_=val_rows[0])
+        nc.sync.dma_start(out=lam_sb[:], in_=lam.rearrange("o (p h) -> (o p) h", h=2))
         nc.sync.dma_start(out=bar_sb[:], in_=bar.rearrange("(p h) o -> p (h o)", h=2))
         nc.sync.dma_start(out=factor_sb[:], in_=slot_factor.rearrange("o (p t) -> (o p) t", t=PACK))
         nc.sync.dma_start(out=reserve_sb[:], in_=reserve.rearrange("(p h) o -> p (h o)", h=2))
@@ -72,35 +89,40 @@ def tile_attend_afterprevious_abovepage_atleast_pl_kernel(
         neg_bar = sb.tile([P, 2], F32, name="neg_bar")
         nc.gpsimd.tensor_scalar(neg_bar[:], bar_sb[:], -1.0 / RUN, 0.0, ALU.mult, ALU.add)
 
+        W = I // HALVES
         key_scales = sb.tile([P, I], U8, name="key_scales", align_bytes=64)
-        key_words = sb.tile([P, I], U16, name="key_words", align_bytes=64)
-        nc.vector.tensor_copy(key_scales[:], key_scale_pool[:].indirect(offsets[:]))
-        nc.vector.tensor_copy(key_words[:], key_word_pool[:].indirect(offsets[:]))
-
+        key_words = [sb.tile([P, W], U16, name="key_words%d" % j, align_bytes=64) for j in range(HALVES)]
         q_bf = [sb.tile([P, P, PACK], BF16, name="q_bf%d" % k, align_bytes=64) for k in range(3)]
         q_codes = [sb.tile([P, P], U32, name="q_codes%d" % k, align_bytes=64) for k in range(3)]
         q_scales = [sb.tile([P, P], U8, name="q_scales%d" % k, align_bytes=64) for k in range(3)]
         q_pairs = q_raw[:].rearrange("p j (m h) -> p h m j", h=2)
+        nc.vector.tensor_copy(key_scales[:], key_scale_pool[:].indirect(offsets[:]))
         nc.gpsimd.memset(q_bf[BEFORE][:, 0, :], 0.0)
         nc.scalar.activation(q_bf[EVEN][:], q_pairs[:, EVEN], ACT.Copy)
         nc.scalar.activation(q_bf[ODD][:], q_pairs[:, ODD], ACT.Copy)
-        nc.gpsimd.tensor_scalar(q_bf[BEFORE][:, 1:, :], q_pairs[:, ODD, : P - 1, :], 1.0, 0.0, ALU.mult, ALU.add)
-        scores = []
+        nc.scalar.activation(q_bf[BEFORE][:, 1:, :], q_pairs[:, ODD, : P - 1, :], ACT.Copy)
         for k in range(3):
             nc.vector.quantize_mx(
                 out=q_codes[k][:].bitcast(FP8X4), scales=q_scales[k][:], in_=q_bf[k][:].rearrange("p m j -> p (m j)")
             )
-            score = bank(k, [P, I], "score%d" % k)
+            if k < HALVES:
+                nc.vector.tensor_copy(
+                    key_words[k][:], key_word_pool[:].indirect(offsets[:, k * W // 16 : (k + 1) * W // 16])
+                )
+        scores = {}
+        passes = [(k, j) for j in range(HALVES) for k in (EVEN, ODD)] + [(BEFORE, j) for j in range(HALVES)]
+        for k, j in passes:
+            score = bank(k + 4 * j, [P, W], "score%d%d" % (k, j))
             nc.tensor.matmul_mx(
                 out=score[:],
                 lhsT=q_codes[k][:].bitcast(FP8X4),
                 lhsT_scale=q_scales[k][:],
-                rhs=key_words[:].bitcast(FP4X4),
-                rhs_scale=key_scales[:],
+                rhs=key_words[j][:].bitcast(FP4X4),
+                rhs_scale=key_scales[:, j * W : (j + 1) * W],
                 start=True,
                 stop=True,
             )
-            scores.append(score)
+            scores[k, j] = score
 
         factor_ps = bank(3, [P, PACK, P], "factor_ps")
         for t in range(PACK):
@@ -113,17 +135,21 @@ def tile_attend_afterprevious_abovepage_atleast_pl_kernel(
         s = per_parity("s", [P, I], F32)
         p = per_parity("p", [P, I], F32)
         run_sum = per_parity("run_sum", [P, G], F32)
-        excess = per_parity("excess", [P, I], F32)
+        level = per_parity("level", [P, G], F32)
+        excess = per_parity("ex", [P, I], F32)
         part = per_parity("part", [P, I], F32)
         part_sum = per_parity("part_sum", [P, 1], F32)
         denom = per_parity("denom", [P, 1], F32)
         recip = per_parity("recip", [P, 1], F32)
-        w_rows = per_parity("w_rows", [P, I], BF16)
-        w_turned = per_parity("w_turned", [P, P, 2], F32)
+        w_rows = per_parity("w", [P, 2, P, 2], BF16)
+        w_turned = per_parity("wt", [P, P, 2], F32)
         w_codes = sb.tile([P, Q], U32, name="w_codes", align_bytes=64)
         w_scales = sb.tile([P, Q], U8, name="w_scales", align_bytes=64)
         previous = {ODD: EVEN, EVEN: BEFORE}
         order = (ODD, EVEN)
+
+        def runs(ap):
+            return ap.rearrange("q (g r) -> q g r", r=RUN)
 
         def turn_words(rows, b, dest, name, copy):
             words = rows[:].bitcast(F32)
@@ -132,54 +158,95 @@ def tile_attend_afterprevious_abovepage_atleast_pl_kernel(
                 nc.tensor.transpose(turned[:, u, :], words[:, u : I // 2 : 2], ident[:])
             copy(dest[:], turned[:].rearrange("s u x -> s x u"))
 
-        for h in order:
-            nc.scalar.activation(th[h][:], scores[previous[h]][:], ACT.Tanh)
-            nc.vector.scalar_tensor_tensor(s[h][:], th[h][:], lam_sb[:, h : h + 1], scores[h][:], ALU.mult, ALU.add)
-        for h in order:
-            nc.scalar.activation(p[h][:], s[h][:], ACT.Exp)
-        for h in order:
-            nc.vector.tensor_reduce(run_sum[h][:], p[h][:].rearrange("q (g r) -> q g r", r=RUN), AX.X, ALU.add)
-        for h in order:
+        def cols(j):
+            return slice(j * W, (j + 1) * W)
+
+        def score_step(h, j):
+            nc.scalar.activation(th[h][:, cols(j)], scores[previous[h], j][:], ACT.Tanh)
             nc.vector.scalar_tensor_tensor(
-                excess[h][:].rearrange("q (g r) -> q g r", r=RUN),
-                run_sum[h][:].unsqueeze(2).to_broadcast([P, G, RUN]),
-                neg_bar[:, h : h + 1],
-                p[h][:].rearrange("q (g r) -> q g r", r=RUN),
-                ALU.mult,
-                ALU.add,
+                s[h][:, cols(j)], th[h][:, cols(j)], lam_sb[:, h : h + 1], scores[h, j][:], ALU.mult, ALU.add
             )
-            nc.scalar.activation(part[h][:], excess[h][:], ACT.Relu, accum_out=part_sum[h][:])
-        for h in order:
-            nc.vector.tensor_tensor(denom[h][:], part_sum[h][:], reserve_sb[:, h : h + 1], ALU.add)
+
+        def exp_step(h, j):
+            nc.scalar.activation(p[h][:, cols(j)], s[h][:, cols(j)], ACT.Exp)
+
+        def sum_step(h, j):
+            nc.vector.tensor_reduce(
+                run_sum[h][:, j * W // RUN : (j + 1) * W // RUN], runs(p[h][:, cols(j)]), AX.X, ALU.add
+            )
+
+        if HALVES == 1:
+            for step in (score_step, exp_step, sum_step):
+                for h in order:
+                    step(h, 0)
+        else:
+            for h in order:
+                for j in range(HALVES):
+                    for step in (score_step, exp_step, sum_step):
+                        step(h, j)
+        for n, h in enumerate(order):
+            if EXCESS[n] == "V":
+                nc.vector.scalar_tensor_tensor(
+                    runs(excess[h][:]),
+                    run_sum[h][:].unsqueeze(2).to_broadcast([P, G, RUN]),
+                    neg_bar[:, h : h + 1],
+                    runs(p[h][:]),
+                    ALU.mult,
+                    ALU.add,
+                )
+            else:
+                nc.vector.tensor_scalar(level[h][:], run_sum[h][:], neg_bar[:, h : h + 1], None, ALU.mult)
+                nc.gpsimd.tensor_tensor(
+                    runs(excess[h][:]), runs(p[h][:]), level[h][:].unsqueeze(2).to_broadcast([P, G, RUN]), ALU.add
+                )
+            if RELU[n] == "S":
+                nc.scalar.activation(part[h][:], excess[h][:], ACT.Relu, accum_out=part_sum[h][:])
+            else:
+                nc.vector.tensor_scalar(
+                    part[h][:], excess[h][:], 0.0, reserve_sb[:, h : h + 1], ALU.max, ALU.add, accum_out=denom[h][:]
+                )
+        for n, h in enumerate(order):
+            if RELU[n] == "S":
+                if DEN == "S":
+                    nc.scalar.activation(denom[h][:], part_sum[h][:], ACT.Identity, bias=reserve_sb[:, h : h + 1])
+                else:
+                    nc.vector.tensor_tensor(denom[h][:], part_sum[h][:], reserve_sb[:, h : h + 1], ALU.add)
             nc.vector.reciprocal(recip[h][:], denom[h][:])
-            nc.vector.scalar_tensor_tensor(
-                w_rows[h][:].rearrange("q (x t) -> q x t", t=PACK),
-                part[h][:].rearrange("q (x t) -> q x t", t=PACK),
-                recip[h][:],
-                factor_ps[:].rearrange("q t x -> q x t"),
-                ALU.mult,
-                ALU.mult,
-            )
-            turn_words(w_rows[h], previous[h] + 1 if h == ODD else BEFORE, w_turned[h], "w_ps%d" % h, nc.scalar.copy if h == ODD else nc.vector.tensor_copy)
+            turned = bank(1 if h == ODD else 2, [P, 2, P], "w_ps%d" % h)
+            for u in range(2):
+                nc.vector.scalar_tensor_tensor(
+                    w_rows[h][:, u],
+                    part[h][:].rearrange("q (x u e) -> q u x e", u=2, e=2)[:, u],
+                    recip[h][:],
+                    factor_ps[:].rearrange("q (u e) x -> q u x e", u=2)[:, u],
+                    ALU.mult,
+                    ALU.mult,
+                )
+                nc.tensor.transpose(
+                    turned[:, u, :], w_rows[h][:, u].rearrange("q x e -> q (x e)").bitcast(F32), ident[:]
+                )
+            copier(WCOPY[n])(w_turned[h][:], turned[:].rearrange("s u x -> s x u"))
             nc.vector.quantize_mx(
                 out=w_codes[:, h * P : (h + 1) * P].bitcast(FP8X4),
                 scales=w_scales[:, h * P : (h + 1) * P],
                 in_=w_turned[h][:].rearrange("s x u -> s (x u)").bitcast(BF16),
             )
 
-        reuse = ["v_rows0", "s%d" % EVEN, "excess%d" % EVEN, "part%d" % EVEN]
-        v_rows = [sb.tile([P, I], BF16, name="v_rows%d" % t, tag=reuse[t], align_bytes=64) for t in range(PACK)]
+        v_rows = [
+            sb.tile([P, I], BF16, name="v_rows%d" % t, tag=HOLD[t] or "v_rows%d" % t, align_bytes=64) for t in range(PACK)
+        ]
         v_turned = [sb.tile([P, P, 2], F32, name="v_turned%d" % t, align_bytes=64) for t in range(PACK)]
         v_codes = [sb.tile([P, P], U32, name="v_codes%d" % t, align_bytes=64) for t in range(PACK)]
         v_scales = [sb.tile([P, P], U8, name="v_scales%d" % t, align_bytes=64) for t in range(PACK)]
-        half = I // 2
         for t in range(PACK):
-            if t == 2:
-                nc.scalar.activation(v_rows[t][:], val_pool[t][:].indirect(offsets[:]), ACT.Copy)
-            else:
-                nc.vector.tensor_copy(v_rows[t][:, :half], val_pool[t][:].indirect(offsets[:, : half // 16]))
-                nc.scalar.activation(v_rows[t][:, half:], val_pool[t][:].indirect(offsets[:, half // 16 :]), ACT.Copy)
-            turn_words(v_rows[t], 4 + t, v_turned[t], "v_ps%d" % t, nc.scalar.copy)
+            n = I // len(GATHER[t])
+            for j, e in enumerate(GATHER[t]):
+                picked = val_pool[t][:].indirect(offsets[:, j * n // 16 : (j + 1) * n // 16])
+                if e == "V":
+                    nc.vector.tensor_copy(v_rows[t][:, j * n : (j + 1) * n], picked)
+                else:
+                    nc.scalar.activation(v_rows[t][:, j * n : (j + 1) * n], picked, ACT.Copy)
+            turn_words(v_rows[t], [7,5,6,4][t], v_turned[t], "v_ps%d" % t, copier(VCOPY[t]))
             nc.vector.quantize_mx(
                 out=v_codes[t][:].bitcast(FP8X4),
                 scales=v_scales[t][:],
@@ -188,30 +255,75 @@ def tile_attend_afterprevious_abovepage_atleast_pl_kernel(
 
         y = sb.tile([P, PACK, Q], F32, name="y")
         out_rows = out_0.rearrange("(p t) q -> t p q", t=PACK)
-        for t in range(PACK):
-            o = bank(t, [P, 2, P], "o%d" % t)
+        use_tenth = "G" in ADDS
+        if use_tenth:
+            for t in range(PACK):
+                nc.gpsimd.tensor_scalar(
+                    floor_tenth[t // 2][:, t % 2, :], floor_sb[t // 2][:, t % 2, :], 0.1, 0.0, ALU.mult, ALU.add
+                )
+
+        def two_terms(above, below, o, f, f_tenth):
+            if use_tenth:
+                nc.vector.tensor_tensor(above, o, f, ALU.max)
+                nc.vector.scalar_tensor_tensor(below, o, 0.1, f_tenth, ALU.mult, ALU.min)
+            else:
+                nc.vector.scalar_tensor_tensor(above, f, 0.1, o, ALU.mult, ALU.add)
+                nc.vector.scalar_tensor_tensor(below, o, 0.1, f, ALU.mult, ALU.add)
+
+        def join(t, above, below):
+            engine = nc.gpsimd if ADDS[t] == "G" else nc.vector
+            dest = y[:, t, :].rearrange("e (m h) -> e m h", h=2)
+            if EARLY and ADDS[t] == "G":
+                dest, above, below = (x.rearrange("e m h -> e h m") for x in (dest, above, below))
+            engine.tensor_tensor(dest, above, below, ALU.add if use_tenth else ALU.max)
+            nc.sync.dma_start(out=out_rows[t], in_=y[:, t, :])
+
+        def product(o, t, c0, c1):
             nc.tensor.matmul_mx(
-                out=o[:].rearrange("e h m -> e (h m)"),
+                out=o,
                 lhsT=v_codes[t][:].bitcast(FP8X4),
                 lhsT_scale=v_scales[t][:],
-                rhs=w_codes[:].bitcast(FP8X4),
-                rhs_scale=w_scales[:],
+                rhs=w_codes[:, c0:c1].bitcast(FP8X4),
+                rhs_scale=w_scales[:, c0:c1],
                 start=True,
                 stop=True,
             )
-            o_nat = o[:].rearrange("e h m -> e m h")
-            f_row = floor_sb[t // 2][:, t % 2, :]
-            nc.gpsimd.tensor_scalar(floor_tenth[t][:], f_row, 0.1, 0.0, ALU.mult, ALU.add)
-            f_nat = f_row.rearrange("e (m h) -> e m h", h=2)
-            f_tenth = floor_tenth[t][:].rearrange("e (m h) -> e m h", h=2)
-            above = sb.tile([P, P, 2], F32, name="above%d" % t)
-            below = sb.tile([P, P, 2], F32, name="below%d" % t)
-            nc.vector.tensor_tensor(above[:], o_nat, f_nat, ALU.max)
-            nc.vector.scalar_tensor_tensor(below[:], o_nat, 0.1, f_tenth, ALU.mult, ALU.min)
-            (nc.gpsimd if t < PACK - 1 else nc.vector).tensor_tensor(
-                y[:, t, :], above[:].rearrange("e m h -> e (m h)"), below[:].rearrange("e m h -> e (m h)"), ALU.add
-            )
-            nc.sync.dma_start(out=out_rows[t], in_=y[:, t, :])
+
+        if EARLY:
+            above = [sb.tile([P, 2, 2, P], F32, name="above%d" % a) for a in range(2)]
+            below = [sb.tile([P, 2, 2, P], F32, name="below%d" % a) for a in range(2)]
+            for h in order:
+                for a in range(2):
+                    o = bank((0 if h == ODD else 4) + a, [P, 2, P], "o%d%d" % (h, a))
+                    for b in range(2):
+                        product(o[:, b, :], 2 * a + b, h * P, (h + 1) * P)
+                    two_terms(
+                        above[a][:, h],
+                        below[a][:, h],
+                        o[:],
+                        floor_sb[a][:].rearrange("e b (m h) -> e h b m", h=2)[:, h],
+                        floor_tenth[a][:].rearrange("e b (m h) -> e h b m", h=2)[:, h],
+                    )
+            for t in range(PACK):
+                join(
+                    t,
+                    above[t // 2][:, :, t % 2, :].rearrange("e h m -> e m h"),
+                    below[t // 2][:, :, t % 2, :].rearrange("e h m -> e m h"),
+                )
+        else:
+            for t in range(PACK):
+                o = bank(t, [P, 2, P], "o%d" % t)
+                product(o[:].rearrange("e h m -> e (h m)"), t, 0, Q)
+                above = sb.tile([P, P, 2], F32, name="above%d" % t)
+                below = sb.tile([P, P, 2], F32, name="below%d" % t)
+                two_terms(
+                    above[:],
+                    below[:],
+                    o[:].rearrange("e h m -> e m h"),
+                    floor_sb[t // 2][:, t % 2, :].rearrange("e (m h) -> e m h", h=2),
+                    floor_tenth[t // 2][:, t % 2, :].rearrange("e (m h) -> e m h", h=2),
+                )
+                join(t, above[:], below[:])
 
         y_bf = sb.tile([P, Q, PACK], BF16, name="y_bf", align_bytes=64)
         y_codes = sb.tile([P, Q], U32, name="y_codes", align_bytes=64)

from contextlib import ExitStack

import concourse.mybir as mybir
from concourse.masks import make_identity

D, T, I, Q, E, G = 512, 2048, 512, 256, 512, 64
RUN = I // G
P = 128
PACK = 4
FLOPS = 2 * D * I * Q + 2 * I * E * Q

F32 = mybir.dt.float32
BF16 = mybir.dt.bfloat16
I32 = mybir.dt.int32
U32 = mybir.dt.uint32
U16 = mybir.dt.uint16
U8 = mybir.dt.uint8
FP8X4 = mybir.dt.float8_e4m3fn_x4
FP4X4 = mybir.dt.float4_e2m1fn_x4
ALU = mybir.AluOpType
ACT = mybir.ActivationFunctionType
AX = mybir.AxisListType

EVEN, ODD, BEFORE = 0, 1, 2
CAST_SPLIT = 160
HALVES = 2
EARLY = False
RELU = "SV"
GATHER = ["VS","S","S","S"]
HOLD = [None,None,None,None]
WCOPY = "VS"
VCOPY = "SVVS"
ADDS = "VVVV"
DEN = "S"
EXCESS = "VV"
KEYS_FIRST = True


def tile_attend_afterprevious_abovepage_atleast_pl_kernel(
    tc, query, keys_words, keys_scales, lam, bar, reserve, slot_factor, vals, floors, offs, out_0, out_1, out_2
):
    nc = tc.nc
    with ExitStack() as ctx:
        sb = ctx.enter_context(tc.tile_pool(name="sb", bufs=1))
        ps = ctx.enter_context(tc.psum_pool(name="ps", bufs=1))

        def bank(b, shape, name):
            return ps.tile(shape, F32, name=name, tag="bank%d" % b)

        def copier(e):
            return nc.scalar.copy if e == "S" else nc.vector.tensor_copy

        offsets = sb.tile([P, I // 16], U16, name="offsets")
        key_scale_pool = sb.tile([P, T], U8, name="key_scale_pool")
        key_word_pool = sb.tile([P, T], U16, name="key_word_pool")
        q_raw = sb.tile([P, PACK, Q], F32, name="q_raw")
        val_pool = [sb.tile([P, T], F32, name="val_pool%d" % t) for t in range(PACK)]
        floor_sb = [sb.tile([P, 2, Q], F32, name="floor_sb%d" % a) for a in range(2)]
        floor_tenth = [sb.tile([P, 2, Q], F32, name="floor_tenth%d" % a) for a in range(2)]
        lam_sb = sb.tile([P, 2], F32, name="lam_sb")
        bar_sb = sb.tile([P, 2], F32, name="bar_sb")
        reserve_sb = sb.tile([P, 2], F32, name="reserve_sb")
        factor_sb = sb.tile([P, PACK], F32, name="factor_sb")
        val_rows = vals.rearrange("(p t) n -> t p n", t=PACK)
        nc.gpsimd.memset(key_scale_pool[:].bitcast(I32), 0)
        nc.sync.dma_start(offsets[:], offs)
        for quad in range(4):
            nc.sync.dma_start(
                out=key_scale_pool[32 * quad : 32 * quad + 4, :].bitcast(I32),
                in_=keys_scales[0, 4 * quad : 4 * quad + 4, :].bitcast(I32),
            )
        for keys_now in (KEYS_FIRST, not KEYS_FIRST):
            if keys_now:
                nc.sync.dma_start(out=key_word_pool[:].bitcast(I32), in_=keys_words[0].bitcast(I32))
            else:
                nc.sync.dma_start(out=q_raw[:], in_=query.rearrange("(p j) q -> p j q", j=PACK))
        nc.sync.dma_start(out=val_pool[0][:], in_=val_rows[0])
        nc.sync.dma_start(out=lam_sb[:], in_=lam.rearrange("o (p h) -> (o p) h", h=2))
        nc.sync.dma_start(out=bar_sb[:], in_=bar.rearrange("(p h) o -> p (h o)", h=2))
        nc.sync.dma_start(out=factor_sb[:], in_=slot_factor.rearrange("o (p t) -> (o p) t", t=PACK))
        nc.sync.dma_start(out=reserve_sb[:], in_=reserve.rearrange("(p h) o -> p (h o)", h=2))
        for t in range(1, PACK):
            nc.sync.dma_start(out=val_pool[t][:], in_=val_rows[t])
        floor_rows = floors.rearrange("(p a b) q -> a p b q", a=2, b=2)
        for a in range(2):
            nc.sync.dma_start(out=floor_sb[a][:], in_=floor_rows[a])
        ident = sb.tile([P, P], F32, name="ident")
        make_identity(nc, ident[:])
        neg_bar = sb.tile([P, 2], F32, name="neg_bar")
        nc.gpsimd.tensor_scalar(neg_bar[:], bar_sb[:], -1.0 / RUN, 0.0, ALU.mult, ALU.add)

        W = I // HALVES
        key_scales = sb.tile([P, I], U8, name="key_scales", align_bytes=64)
        key_words = [sb.tile([P, W], U16, name="key_words%d" % j, align_bytes=64) for j in range(HALVES)]
        q_bf = [sb.tile([P, P, PACK], BF16, name="q_bf%d" % k, align_bytes=64) for k in range(3)]
        q_codes = [sb.tile([P, P], U32, name="q_codes%d" % k, align_bytes=64) for k in range(3)]
        q_scales = [sb.tile([P, P], U8, name="q_scales%d" % k, align_bytes=64) for k in range(3)]
        q_pairs = q_raw[:].rearrange("p j (m h) -> p h m j", h=2)
        nc.vector.tensor_copy(key_scales[:], key_scale_pool[:].indirect(offsets[:]))
        nc.gpsimd.memset(q_bf[BEFORE][:, 0, :], 0.0)
        nc.scalar.activation(q_bf[EVEN][:], q_pairs[:, EVEN], ACT.Copy)
        nc.scalar.activation(q_bf[ODD][:], q_pairs[:, ODD], ACT.Copy)
        nc.scalar.activation(q_bf[BEFORE][:, 1:, :], q_pairs[:, ODD, : P - 1, :], ACT.Copy)
        for k in range(3):
            nc.vector.quantize_mx(
                out=q_codes[k][:].bitcast(FP8X4), scales=q_scales[k][:], in_=q_bf[k][:].rearrange("p m j -> p (m j)")
            )
            if k < HALVES:
                nc.vector.tensor_copy(
                    key_words[k][:], key_word_pool[:].indirect(offsets[:, k * W // 16 : (k + 1) * W // 16])
                )
        scores = {}
        passes = [(k, j) for j in range(HALVES) for k in (EVEN, ODD)] + [(BEFORE, j) for j in range(HALVES)]
        for k, j in passes:
            score = bank(k + 4 * j, [P, W], "score%d%d" % (k, j))
            nc.tensor.matmul_mx(
                out=score[:],
                lhsT=q_codes[k][:].bitcast(FP8X4),
                lhsT_scale=q_scales[k][:],
                rhs=key_words[j][:].bitcast(FP4X4),
                rhs_scale=key_scales[:, j * W : (j + 1) * W],
                start=True,
                stop=True,
            )
            scores[k, j] = score

        factor_ps = bank(3, [P, PACK, P], "factor_ps")
        for t in range(PACK):
            nc.tensor.transpose(factor_ps[:, t, :], factor_sb[:, t : t + 1].to_broadcast([P, P]), ident[:])

        def per_parity(name, shape, dtype):
            return [sb.tile(shape, dtype, name="%s%d" % (name, h), tag="%s%d" % (name, h), align_bytes=64) for h in range(2)]

        th = per_parity("th", [P, I], F32)
        s = per_parity("s", [P, I], F32)
        p = per_parity("p", [P, I], F32)
        run_sum = per_parity("run_sum", [P, G], F32)
        level = per_parity("level", [P, G], F32)
        excess = per_parity("ex", [P, I], F32)
        part = per_parity("part", [P, I], F32)
        part_sum = per_parity("part_sum", [P, 1], F32)
        denom = per_parity("denom", [P, 1], F32)
        recip = per_parity("recip", [P, 1], F32)
        w_rows = per_parity("w", [P, 2, P, 2], BF16)
        w_turned = per_parity("wt", [P, P, 2], F32)
        w_codes = sb.tile([P, Q], U32, name="w_codes", align_bytes=64)
        w_scales = sb.tile([P, Q], U8, name="w_scales", align_bytes=64)
        previous = {ODD: EVEN, EVEN: BEFORE}
        order = (ODD, EVEN)

        def runs(ap):
            return ap.rearrange("q (g r) -> q g r", r=RUN)

        def turn_words(rows, b, dest, name, copy):
            words = rows[:].bitcast(F32)
            turned = bank(b, [P, 2, P], name)
            for u in range(2):
                nc.tensor.transpose(turned[:, u, :], words[:, u : I // 2 : 2], ident[:])
            copy(dest[:], turned[:].rearrange("s u x -> s x u"))

        def cols(j):
            return slice(j * W, (j + 1) * W)

        def score_step(h, j):
            nc.scalar.activation(th[h][:, cols(j)], scores[previous[h], j][:], ACT.Tanh)
            nc.vector.scalar_tensor_tensor(
                s[h][:, cols(j)], th[h][:, cols(j)], lam_sb[:, h : h + 1], scores[h, j][:], ALU.mult, ALU.add
            )

        def exp_step(h, j):
            nc.scalar.activation(p[h][:, cols(j)], s[h][:, cols(j)], ACT.Exp)

        def sum_step(h, j):
            nc.vector.tensor_reduce(
                run_sum[h][:, j * W // RUN : (j + 1) * W // RUN], runs(p[h][:, cols(j)]), AX.X, ALU.add
            )

        if HALVES == 1:
            for step in (score_step, exp_step, sum_step):
                for h in order:
                    step(h, 0)
        else:
            for h in order:
                for j in range(HALVES):
                    for step in (score_step, exp_step, sum_step):
                        step(h, j)
        for n, h in enumerate(order):
            if EXCESS[n] == "V":
                nc.vector.scalar_tensor_tensor(
                    runs(excess[h][:]),
                    run_sum[h][:].unsqueeze(2).to_broadcast([P, G, RUN]),
                    neg_bar[:, h : h + 1],
                    runs(p[h][:]),
                    ALU.mult,
                    ALU.add,
                )
            else:
                nc.vector.tensor_scalar(level[h][:], run_sum[h][:], neg_bar[:, h : h + 1], None, ALU.mult)
                nc.gpsimd.tensor_tensor(
                    runs(excess[h][:]), runs(p[h][:]), level[h][:].unsqueeze(2).to_broadcast([P, G, RUN]), ALU.add
                )
            if RELU[n] == "S":
                nc.scalar.activation(part[h][:], excess[h][:], ACT.Relu, accum_out=part_sum[h][:])
            else:
                nc.vector.tensor_scalar(
                    part[h][:], excess[h][:], 0.0, reserve_sb[:, h : h + 1], ALU.max, ALU.add, accum_out=denom[h][:]
                )
        for n, h in enumerate(order):
            if RELU[n] == "S":
                if DEN == "S":
                    nc.scalar.activation(denom[h][:], part_sum[h][:], ACT.Identity, bias=reserve_sb[:, h : h + 1])
                else:
                    nc.vector.tensor_tensor(denom[h][:], part_sum[h][:], reserve_sb[:, h : h + 1], ALU.add)
            nc.vector.reciprocal(recip[h][:], denom[h][:])
            turned = bank(1 if h == ODD else 2, [P, 2, P], "w_ps%d" % h)
            for u in range(2):
                nc.vector.scalar_tensor_tensor(
                    w_rows[h][:, u],
                    part[h][:].rearrange("q (x u e) -> q u x e", u=2, e=2)[:, u],
                    recip[h][:],
                    factor_ps[:].rearrange("q (u e) x -> q u x e", u=2)[:, u],
                    ALU.mult,
                    ALU.mult,
                )
                nc.tensor.transpose(
                    turned[:, u, :], w_rows[h][:, u].rearrange("q x e -> q (x e)").bitcast(F32), ident[:]
                )
            copier(WCOPY[n])(w_turned[h][:], turned[:].rearrange("s u x -> s x u"))
            nc.vector.quantize_mx(
                out=w_codes[:, h * P : (h + 1) * P].bitcast(FP8X4),
                scales=w_scales[:, h * P : (h + 1) * P],
                in_=w_turned[h][:].rearrange("s x u -> s (x u)").bitcast(BF16),
            )

        v_rows = [
            sb.tile([P, I], BF16, name="v_rows%d" % t, tag=HOLD[t] or "v_rows%d" % t, align_bytes=64) for t in range(PACK)
        ]
        v_turned = [sb.tile([P, P, 2], F32, name="v_turned%d" % t, align_bytes=64) for t in range(PACK)]
        v_codes = [sb.tile([P, P], U32, name="v_codes%d" % t, align_bytes=64) for t in range(PACK)]
        v_scales = [sb.tile([P, P], U8, name="v_scales%d" % t, align_bytes=64) for t in range(PACK)]
        for t in range(PACK):
            n = I // len(GATHER[t])
            for j, e in enumerate(GATHER[t]):
                picked = val_pool[t][:].indirect(offsets[:, j * n // 16 : (j + 1) * n // 16])
                if e == "V":
                    nc.vector.tensor_copy(v_rows[t][:, j * n : (j + 1) * n], picked)
                else:
                    nc.scalar.activation(v_rows[t][:, j * n : (j + 1) * n], picked, ACT.Copy)
            turn_words(v_rows[t], [7,5,6,4][t], v_turned[t], "v_ps%d" % t, copier(VCOPY[t]))
            nc.vector.quantize_mx(
                out=v_codes[t][:].bitcast(FP8X4),
                scales=v_scales[t][:],
                in_=v_turned[t][:].rearrange("s x u -> s (x u)").bitcast(BF16),
            )

        y = sb.tile([P, PACK, Q], F32, name="y")
        out_rows = out_0.rearrange("(p t) q -> t p q", t=PACK)
        use_tenth = "G" in ADDS
        if use_tenth:
            for t in range(PACK):
                nc.gpsimd.tensor_scalar(
                    floor_tenth[t // 2][:, t % 2, :], floor_sb[t // 2][:, t % 2, :], 0.1, 0.0, ALU.mult, ALU.add
                )

        def two_terms(above, below, o, f, f_tenth):
            if use_tenth:
                nc.vector.tensor_tensor(above, o, f, ALU.max)
                nc.vector.scalar_tensor_tensor(below, o, 0.1, f_tenth, ALU.mult, ALU.min)
            else:
                nc.vector.scalar_tensor_tensor(above, f, 0.1, o, ALU.mult, ALU.add)
                nc.vector.scalar_tensor_tensor(below, o, 0.1, f, ALU.mult, ALU.add)

        def join(t, above, below):
            engine = nc.gpsimd if ADDS[t] == "G" else nc.vector
            dest = y[:, t, :].rearrange("e (m h) -> e m h", h=2)
            if EARLY and ADDS[t] == "G":
                dest, above, below = (x.rearrange("e m h -> e h m") for x in (dest, above, below))
            engine.tensor_tensor(dest, above, below, ALU.add if use_tenth else ALU.max)
            nc.sync.dma_start(out=out_rows[t], in_=y[:, t, :])

        def product(o, t, c0, c1):
            nc.tensor.matmul_mx(
                out=o,
                lhsT=v_codes[t][:].bitcast(FP8X4),
                lhsT_scale=v_scales[t][:],
                rhs=w_codes[:, c0:c1].bitcast(FP8X4),
                rhs_scale=w_scales[:, c0:c1],
                start=True,
                stop=True,
            )

        if EARLY:
            above = [sb.tile([P, 2, 2, P], F32, name="above%d" % a) for a in range(2)]
            below = [sb.tile([P, 2, 2, P], F32, name="below%d" % a) for a in range(2)]
            for h in order:
                for a in range(2):
                    o = bank((0 if h == ODD else 4) + a, [P, 2, P], "o%d%d" % (h, a))
                    for b in range(2):
                        product(o[:, b, :], 2 * a + b, h * P, (h + 1) * P)
                    two_terms(
                        above[a][:, h],
                        below[a][:, h],
                        o[:],
                        floor_sb[a][:].rearrange("e b (m h) -> e h b m", h=2)[:, h],
                        floor_tenth[a][:].rearrange("e b (m h) -> e h b m", h=2)[:, h],
                    )
            for t in range(PACK):
                join(
                    t,
                    above[t // 2][:, :, t % 2, :].rearrange("e h m -> e m h"),
                    below[t // 2][:, :, t % 2, :].rearrange("e h m -> e m h"),
                )
        else:
            for t in range(PACK):
                o = bank(t, [P, 2, P], "o%d" % t)
                product(o[:].rearrange("e h m -> e (h m)"), t, 0, Q)
                above = sb.tile([P, P, 2], F32, name="above%d" % t)
                below = sb.tile([P, P, 2], F32, name="below%d" % t)
                two_terms(
                    above[:],
                    below[:],
                    o[:].rearrange("e h m -> e m h"),
                    floor_sb[t // 2][:, t % 2, :].rearrange("e (m h) -> e m h", h=2),
                    floor_tenth[t // 2][:, t % 2, :].rearrange("e (m h) -> e m h", h=2),
                )
                join(t, above[:], below[:])

        y_bf = sb.tile([P, Q, PACK], BF16, name="y_bf", align_bytes=64)
        y_codes = sb.tile([P, Q], U32, name="y_codes", align_bytes=64)
        y_scales = sb.tile([P, Q], U8, name="y_scales", align_bytes=64)
        y_cols = y[:].rearrange("p t q -> p q t")
        nc.vector.tensor_copy(y_bf[:, :CAST_SPLIT, :], y_cols[:, :CAST_SPLIT, :])
        nc.scalar.copy(y_bf[:, CAST_SPLIT:, :], y_cols[:, CAST_SPLIT:, :])
        nc.vector.quantize_mx(
            out=y_codes[:].bitcast(FP8X4), scales=y_scales[:], in_=y_bf[:].rearrange("p q t -> p (q t)")
        )
        nc.sync.dma_start(out=out_1[0].rearrange("p c r -> p (c r)").bitcast(I32), in_=y_codes[:].bitcast(I32))
        for quad in range(4):
            queue = nc.scalar if quad % 2 == 0 else nc.sync
            queue.dma_start(
                out=out_2[0, 4 * quad : 4 * quad + 4, :].bitcast(I32),
                in_=y_scales[32 * quad : 32 * quad + 4, :].bitcast(I32),
            )
